import numpy as np
import ml_dtypes


def mxq(x, axis, fmt="e4m3"):
    dtype, down = {"e4m3": (ml_dtypes.float8_e4m3fn, 7), "e5m2": (ml_dtypes.float8_e5m2, 14)}[fmt]
    v = np.moveaxis(np.asarray(x, np.float32).astype(ml_dtypes.bfloat16).astype(np.float64), axis, -1)
    blocks = v.reshape(v.shape[:-1] + (-1, 32))
    amax = np.abs(blocks).max(-1, keepdims=True)
    byte = np.maximum(np.where(amax > 0, np.frexp(amax)[1] - 1 + 127, 0) - down, 1)
    scale = np.exp2(byte - 127.0)
    codes = (blocks / scale).astype(np.float32).astype(dtype).astype(np.float64)
    return np.moveaxis((codes * scale).reshape(v.shape), -1, axis)


WIDE = False


def mx_kscale(k):
    if not WIDE:
        return np.ones(k)
    levels = np.array([10, -10, 5, -5, 0])
    if k % 512:
        return np.exp2(np.random.permutation(np.resize(levels, k // 32))).repeat(32)
    a = np.empty((k // 512, 16))
    for p in range(k // 512):
        a[p, :8] = np.random.permutation(np.resize(levels, 8))
        for g in range(8):
            far = levels[np.abs(levels - a[p, g]) >= 10]
            a[p, g + 8] = far[np.random.randint(len(far))]
    return np.exp2(a.ravel()).repeat(32)


def f64(x):
    return np.asarray(x).astype(np.float64)


def striped(idx):
    return np.tile(np.asarray(idx).reshape(-1, 16).T, (8, 1)).astype(np.uint16)


def unstriped(offs):
    return offs[:16].T.reshape(-1).astype(np.int64)


E2M1 = np.array([0.0, 0.5, 1.0, 1.5, 2.0, 3.0, 4.0, 6.0, -0.0, -0.5, -1.0, -1.5, -2.0, -3.0, -4.0, -6.0])


def pack_weight(w, fmt):
    k, n = w.shape
    w = f64(np.asarray(w, np.float32).astype(ml_dtypes.bfloat16)).reshape(k // 32, 32, n)
    amax = np.abs(w).max(1)
    if fmt == "e4m3":
        byte = np.frexp(amax)[1] - 1 + 127 - 7
    else:
        mant, ex = np.frexp(amax / 6.0)
        byte = np.where(mant > 0.5, ex, ex - 1) + 127
    byte = np.clip(np.where(amax > 0, byte, 1), 1, 254)
    scaled = (w * np.exp2(127.0 - byte)[:, None, :]).reshape(k, n).astype(np.float32)
    by_word = np.ascontiguousarray(scaled.reshape(k // 512, 128, 4, n).transpose(0, 1, 3, 2))
    if fmt == "e4m3":
        words = by_word.astype(ml_dtypes.float8_e4m3fn).view(np.uint8)
    else:
        c = by_word.astype(ml_dtypes.float4_e2m1fn).view(np.uint8) & 0xF
        words = (c[..., 0::2] | (c[..., 1::2] << 4)).reshape(k // 512, 128, 2 * n)
    return np.ascontiguousarray(words), np.ascontiguousarray(byte.astype(np.uint8).reshape(k // 512, 16, n))


def unpack_weight(words, scales, fmt):
    g, _, n = scales.shape
    words = np.ascontiguousarray(words).reshape(g, 128, n, -1)
    if fmt == "e4m3":
        vals = words.view(ml_dtypes.float8_e4m3fn).astype(np.float64)
    else:
        nib = np.empty((g, 128, n, 4), np.uint8)
        nib[..., 0::2] = words & 0xF
        nib[..., 1::2] = words >> 4
        vals = E2M1[nib]
    vals = vals * np.repeat(np.exp2(scales.astype(np.float64) - 127.0), 8, axis=1)[..., None]
    return vals.transpose(0, 1, 3, 2).reshape(g * 512, n)


def bf(x):
    return np.asarray(x, np.float32).astype(ml_dtypes.bfloat16)


def planes(Y):
    r, m = Y.shape
    b = f64(bf(Y)).reshape(r // 32, 32, m)
    amax = np.abs(b).max(1)
    byte = np.clip(np.where(amax > 0, np.frexp(amax)[1] - 1 + 127 - 7, 1), 1, 254)
    codes = (b * np.exp2(127.0 - byte)[:, None, :]).reshape(r, m).astype(np.float32).astype(ml_dtypes.float8_e4m3fn).view(np.uint8)
    words = codes.reshape(r // 512, 128, 4, m).transpose(0, 1, 3, 2)
    return np.ascontiguousarray(words), np.ascontiguousarray(byte.astype(np.uint8).reshape(r // 512, 16, m))


K, T, J, N = 1024, 2048, 512, 512


def setup_inputs():
    n = np.random.standard_normal
    idx = np.random.permutation(T)[:J]
    idx2 = np.random.permutation(T)[:J]
    fk = mx_kscale(K)
    wap = pack_weight(n((K, N)) * 1 / np.sqrt(K) * fk[:, None], "e2m1")
    wbp = pack_weight(n((K, N)) * 1 / np.sqrt(K) * fk[:, None], "e4m3")
    return {
        "xt": (n((K, T)) * np.random.uniform(0.3, 1.7, (1, T)) / fk[:, None]).astype(np.float32),
        "wa_words": wap[0],
        "wa_scales": wap[1],
        "wb_words": wbp[0],
        "wb_scales": wbp[1],
        "bi": (1.0 * n((1, N))).astype(np.float32),
        "offs": striped(idx),
        "offs2": striped(idx2),
    }


def reference(xt, wa_words, wa_scales, wb_words, wb_scales, bi, offs, offs2):
    idx = unstriped(offs)
    idx2 = unstriped(offs2)
    wau = unpack_weight(wa_words, wa_scales, "e2m1")
    wbu = unpack_weight(wb_words, wb_scales, "e4m3")
    xtidxq = mxq(f64(xt)[:, idx], 0, "e4m3")
    a = xtidxq.T @ wau
    xtidx2q = mxq(f64(xt)[:, idx2], 0, "e4m3")
    b0 = xtidx2q.T @ wbu
    b = b0 + f64(bi)
    s = np.tanh(2.0 * np.mean((a + f64(bi)) * b, axis=1, keepdims=True))
    y = a + s * b
    words, scales = planes(y)
    return y, words, scales

@@ -1,0 +1,210 @@
+from contextlib import ExitStack
+
+import concourse.mybir as mybir
+from concourse.masks import make_identity
+
+K, T, J, N = 1024, 2048, 512, 512
+FLOPS = 2 * 2 * K * J * N
+
+F32 = mybir.dt.float32
+BF16 = mybir.dt.bfloat16
+I32 = mybir.dt.int32
+U32 = mybir.dt.uint32
+U16 = mybir.dt.uint16
+U8 = mybir.dt.uint8
+FP8X4 = mybir.dt.float8_e4m3fn_x4
+FP4X4 = mybir.dt.float4_e2m1fn_x4
+ACT = mybir.ActivationFunctionType
+ALU = mybir.AluOpType
+
+P = 128
+PACK = 4
+PASSES = K // (P * PACK)
+HALF = N // 2
+
+WIDE = [(0, 1024, 768), (1024, 1024, 768)]
+LAST = [(0, 1024, 768), (1024, 512, 128), (1536, 512, 160)]
+
+
+def tile_moe_experts_by_agreement_pl_kernel(tc, xt, wa_words, wa_scales, wb_words, wb_scales, bi, offs, offs2, out_0, out_1, out_2):
+    nc = tc.nc
+    with ExitStack() as ctx:
+        keep = ctx.enter_context(tc.tile_pool(name="keep", bufs=1))
+        psum = ctx.enter_context(tc.psum_pool(name="psum", bufs=1))
+
+        x_rows = xt.rearrange("(g p u e) t -> g u p e t", g=PASSES, p=P, u=2, e=2)
+
+        lists = {"a": keep.tile([P, J // 16], U16, name="list_a"), "b": keep.tile([P, J // 16], U16, name="list_b")}
+        wa = keep.tile([P, PASSES, 2 * N], U8, name="wa", align_bytes=64)
+        wb = keep.tile([P, PASSES, N], U32, name="wb", align_bytes=64)
+        sa = keep.tile([P, PASSES, N], U8, name="sa", align_bytes=64)
+        sb = keep.tile([P, N], U8, name="sb", align_bytes=64)
+        bias_col = keep.tile([P, PACK], F32, name="bias_col")
+        bias = keep.tile([P, N], F32, name="bias")
+        ident = keep.tile([P, P], F32, name="ident")
+        warm = keep.tile([P, 8], F32, name="warm")
+
+        nc.vector.memset(warm[:], 0.0)
+        nc.scalar.activation(warm[:, 0:1], warm[:, 1:2], ACT.Tanh)
+        nc.vector.memset(sa[:].rearrange("p g n -> p (g n)").bitcast(I32), 0)
+        nc.vector.memset(sb[:].bitcast(I32), 0)
+        make_identity(nc, ident[:])
+
+        pairs = {}
+        staged = {}
+
+        def load_x(g, u, chunk):
+            c0, width, share = chunk
+            raw = keep.tile([P, 2, width], F32, name="raw_%d%d_%d" % (g, u, c0))
+            nc.sync.dma_start(out=raw[:], in_=x_rows[g, u][:, :, c0 : c0 + width])
+            staged[g, u, c0] = raw
+
+        def cast_x(g, u, chunk):
+            c0, width, share = chunk
+            if (g, u) not in pairs:
+                pairs[g, u] = keep.tile([P, T], F32, name="pair_%d%d" % (g, u))
+            dst = pairs[g, u][:].bitcast(BF16).rearrange("p (t e) -> p t e", e=2)
+            src = staged[g, u, c0][:].rearrange("p e t -> p t e")
+            nc.scalar.activation(dst[:, c0 : c0 + share, :], src[:, :share, :], ACT.Copy)
+            nc.vector.tensor_copy(dst[:, c0 + share : c0 + width, :], src[:, share:, :])
+
+        gathered = {(s, g): keep.tile([P, 2, J], F32, name="gathered_%s%d" % (s, g)) for s in "ab" for g in range(PASSES)}
+        woven = {(s, g): keep.tile([P, 2 * J], F32, name="woven_%s%d" % (s, g), align_bytes=64) for s in "ab" for g in range(PASSES)}
+        codes = {(s, g): keep.tile([P, J], U32, name="codes_%s%d" % (s, g), align_bytes=64) for s in "ab" for g in range(PASSES)}
+        scales = {(s, g): keep.tile([P, J], U8, name="scales_%s%d" % (s, g), align_bytes=64) for s in "ab" for g in range(PASSES)}
+
+        def gather(s, g, u):
+            nc.vector.tensor_copy(gathered[s, g][:, u, :], pairs[g, u][:].indirect(lists[s][:]))
+
+        def weave(s, g):
+            dst = woven[s, g][:].rearrange("p (t m u) -> p m u t", t=PACK, u=2)
+            src = gathered[s, g][:].rearrange("p u (m t) -> p m u t", t=PACK)
+            if g == 0:
+                nc.vector.tensor_copy(dst, src)
+            else:
+                nc.scalar.copy(dst, src)
+
+        def quantize(s, g, c0, c1):
+            nc.vector.quantize_mx(
+                out=codes[s, g][:, c0:c1].bitcast(FP8X4),
+                scales=scales[s, g][:, c0:c1],
+                in_=woven[s, g][:].bitcast(BF16)[:, PACK * c0 : PACK * c1],
+            )
+
+        def load_words(s, g):
+            if s == "a":
+                nc.sync.dma_start(out=wa[:, g, :].bitcast(I32), in_=wa_words[g].bitcast(I32))
+            else:
+                nc.sync.dma_start(out=wb[:, g, :].bitcast(I32), in_=wb_words[g].rearrange("p n t -> p (n t)").bitcast(I32))
+
+        def load_scales(q):
+            rows = slice(4 * q, 4 * q + 4)
+            nc.sync.dma_start(out=sa[32 * q : 32 * q + 4, :, :].bitcast(I32), in_=wa_scales[:, rows, :].rearrange("g r n -> r g n").bitcast(I32))
+            nc.sync.dma_start(out=sb[32 * q + 4 : 32 * q + 12, :].bitcast(I32), in_=wb_scales[:, rows, :].bitcast(I32))
+
+        load_x(0, 0, WIDE[0])
+        load_x(0, 0, WIDE[1])
+        nc.sync.dma_start(bias_col[:], bi.rearrange("o (p c) -> (o p) c", c=PACK))
+        nc.sync.dma_start(lists["b"][:], offs2)
+        nc.sync.dma_start(lists["a"][:], offs)
+        load_x(0, 1, WIDE[0])
+        load_x(0, 1, WIDE[1])
+        load_scales(0)
+        load_scales(1)
+        load_x(1, 0, WIDE[0])
+        load_x(1, 0, WIDE[1])
+        load_scales(2)
+        load_scales(3)
+        load_x(1, 1, LAST[0])
+        load_words("a", 0)
+        load_x(1, 1, LAST[1])
+        load_x(1, 1, LAST[2])
+        load_words("b", 0)
+        load_words("b", 1)
+        load_words("a", 1)
+
+        spread = psum.tile([P, PACK, P], F32, name="spread", tag="a0")
+        for c in range(PACK):
+            nc.tensor.transpose(spread[:, c, :], bias_col[:, c : c + 1].to_broadcast([P, P]), ident[:])
+        nc.scalar.activation(bias[:].rearrange("m (p c) -> m p c", c=PACK), spread[:].rearrange("m c p -> m p c"), ACT.Copy)
+
+        acc = {(s, t): psum.tile([P, N], F32, name="acc_%s%d" % (s, t), tag="%s%d" % (s, t)) for s in "ab" for t in range(PACK)}
+
+        def product(s, g, t):
+            cols = slice(t * P, (t + 1) * P)
+            if s == "a":
+                rhs, rhs_scale = wa[:, g, :].bitcast(FP4X4), sa[:, g, :]
+            else:
+                rhs, rhs_scale = wb[:, g, :].bitcast(FP8X4), sb[4 + 4 * g :, :]
+            nc.tensor.matmul_mx(
+                out=acc[s, t][:],
+                lhsT=codes[s, g][:, cols].bitcast(FP8X4),
+                lhsT_scale=scales[s, g][:, cols],
+                rhs=rhs,
+                rhs_scale=rhs_scale,
+                start=(g == 0),
+                stop=(g == PASSES - 1),
+            )
+
+        for g in range(PASSES):
+            for u in range(2):
+                for chunk in LAST if (g, u) == (1, 1) else WIDE:
+                    cast_x(g, u, chunk)
+                gather("b", g, u)
+                gather("a", g, u)
+            if g == 0:
+                weave("a", 0)
+                weave("b", 0)
+                quantize("a", 0, 0, J)
+                quantize("b", 0, 0, J)
+                for s in "ab":
+                    for t in range(PACK):
+                        product(s, 0, t)
+        weave("b", 1)
+        weave("a", 1)
+        quantize("b", 1, 0, J // 2)
+        quantize("b", 1, J // 2, J)
+        for t in range(PACK):
+            product("b", 1, t)
+        quantize("a", 1, 0, J)
+        for t in range(PACK):
+            product("a", 1, t)
+
+        b_rows = [keep.tile([P, N], F32, name="b_rows%d" % t) for t in range(PACK)]
+        bias_b = [keep.tile([P, N], F32, name="bias_b%d" % t) for t in range(PACK)]
+        y = keep.tile([P, PACK, N], F32, name="y")
+        sum_ab = keep.tile([P, PACK], F32, name="sum_ab")
+        sum_bias_b = keep.tile([P, PACK], F32, name="sum_bias_b")
+        gate = keep.tile([P, PACK], F32, name="gate")
+        for t in range(PACK):
+            nc.vector.tensor_tensor(b_rows[t][:], acc["b", t][:], bias[:], ALU.add)
+            nc.gpsimd.tensor_tensor(bias_b[t][:], b_rows[t][:], bias[:], ALU.mult)
+            nc.scalar.activation(bias_b[t][:], bias_b[t][:], ACT.Copy, scale=2.0 / N, accum_out=sum_bias_b[:, t : t + 1])
+        for t in range(PACK):
+            nc.vector.scalar_tensor_tensor(y[:, t, :], acc["a", t][:], 2.0 / N, b_rows[t][:], ALU.mult, ALU.mult, accum_out=sum_ab[:, t : t + 1])
+            nc.scalar.activation(gate[:, t : t + 1], sum_ab[:, t : t + 1], ACT.Tanh, bias=sum_bias_b[:, t : t + 1])
+
+        y_bf = keep.tile([P, N * PACK], BF16, name="y_bf", align_bytes=64)
+        y_codes = keep.tile([P, N], U32, name="y_codes", align_bytes=64)
+        y_scales = keep.tile([P, N], U8, name="y_scales", align_bytes=64)
+        out_rows = out_0.rearrange("(p t) n -> p t n", t=PACK)
+        out_words = out_1[0].rearrange("p n t -> p (n t)").bitcast(I32)
+        for h in range(2):
+            cols = slice(h * HALF, (h + 1) * HALF)
+            for t in range(PACK):
+                nc.vector.scalar_tensor_tensor(y[:, t, cols], b_rows[t][:, cols], gate[:, t : t + 1], acc["a", t][:, cols], ALU.mult, ALU.add)
+                if t % 2 == 1:
+                    nc.sync.dma_start(out=out_rows[:, t - 1 : t + 1, cols], in_=y[:, t - 1 : t + 1, cols])
+            dst = y_bf[:, PACK * h * HALF : PACK * (h + 1) * HALF].rearrange("p (c i t) -> p c t i", i=4, t=PACK)
+            src = y[:, :, cols].rearrange("p t (c i) -> p c t i", i=4)
+            if h == 0:
+                nc.scalar.activation(dst, src, ACT.Copy)
+            else:
+                nc.vector.tensor_copy(dst, src)
+        for h in range(2):
+            cols = slice(h * HALF, (h + 1) * HALF)
+            nc.vector.quantize_mx(out=y_codes[:, cols].bitcast(FP8X4), scales=y_scales[:, cols], in_=y_bf[:, PACK * h * HALF : PACK * (h + 1) * HALF])
+            nc.sync.dma_start(out=out_words[:, cols], in_=y_codes[:, cols].bitcast(I32))
+        for q in range(4):
+            queue = nc.scalar if q % 2 == 0 else nc.sync
+            queue.dma_start(out=out_2[0, 4 * q : 4 * q + 4, :].bitcast(I32), in_=y_scales[32 * q : 32 * q + 4, :].bitcast(I32))

@@ -22,8 +22,13 @@ PACK = 4
 PASSES = K // (P * PACK)
 HALF = N // 2
 
-WIDE = [(0, 1024, 768), (1024, 1024, 768)]
-LAST = [(0, 1024, 768), (1024, 512, 128), (1536, 512, 160)]
+CHUNKS = {
+    (0, 0): [(0, 2048, 704)],
+    (0, 1): [(0, 1024, 1024), (1024, 1024, 352)],
+    (1, 0): [(0, 512, 512), (512, 512, 512), (1024, 512, 512), (1536, 512, 512)],
+    (1, 1): [(0, 512, 512), (512, 512, 512), (1024, 768, 320), (1792, 256, 0)],
+}
+WEAVE_SCALAR = 88
 
 
 def tile_moe_experts_by_agreement_pl_kernel(tc, xt, wa_words, wa_scales, wb_words, wb_scales, bi, offs, offs2, out_0, out_1, out_2):
@@ -65,8 +70,10 @@ def tile_moe_experts_by_agreement_pl_kernel(tc, xt, wa_words, wa_scales, wb_word
                 pairs[g, u] = keep.tile([P, T], F32, name="pair_%d%d" % (g, u))
             dst = pairs[g, u][:].bitcast(BF16).rearrange("p (t e) -> p t e", e=2)
             src = staged[g, u, c0][:].rearrange("p e t -> p t e")
-            nc.scalar.activation(dst[:, c0 : c0 + share, :], src[:, :share, :], ACT.Copy)
-            nc.vector.tensor_copy(dst[:, c0 + share : c0 + width, :], src[:, share:, :])
+            if share > 0:
+                nc.scalar.activation(dst[:, c0 : c0 + share, :], src[:, :share, :], ACT.Copy)
+            if share < width:
+                nc.vector.tensor_copy(dst[:, c0 + share : c0 + width, :], src[:, share:, :])
 
         gathered = {(s, g): keep.tile([P, 2, J], F32, name="gathered_%s%d" % (s, g)) for s in "ab" for g in range(PASSES)}
         woven = {(s, g): keep.tile([P, 2 * J], F32, name="woven_%s%d" % (s, g), align_bytes=64) for s in "ab" for g in range(PASSES)}
@@ -76,13 +83,13 @@ def tile_moe_experts_by_agreement_pl_kernel(tc, xt, wa_words, wa_scales, wb_word
         def gather(s, g, u):
             nc.vector.tensor_copy(gathered[s, g][:, u, :], pairs[g, u][:].indirect(lists[s][:]))
 
-        def weave(s, g):
+        def weave(s, g, m_scalar):
             dst = woven[s, g][:].rearrange("p (t m u) -> p m u t", t=PACK, u=2)
             src = gathered[s, g][:].rearrange("p u (m t) -> p m u t", t=PACK)
-            if g == 0:
-                nc.vector.tensor_copy(dst, src)
-            else:
-                nc.scalar.copy(dst, src)
+            if m_scalar > 0:
+                nc.scalar.copy(dst[:, :m_scalar], src[:, :m_scalar])
+            if m_scalar < P:
+                nc.vector.tensor_copy(dst[:, m_scalar:], src[:, m_scalar:])
 
         def quantize(s, g, c0, c1):
             nc.vector.quantize_mx(
@@ -102,23 +109,22 @@ def tile_moe_experts_by_agreement_pl_kernel(tc, xt, wa_words, wa_scales, wb_word
             nc.sync.dma_start(out=sa[32 * q : 32 * q + 4, :, :].bitcast(I32), in_=wa_scales[:, rows, :].rearrange("g r n -> r g n").bitcast(I32))
             nc.sync.dma_start(out=sb[32 * q + 4 : 32 * q + 12, :].bitcast(I32), in_=wb_scales[:, rows, :].bitcast(I32))
 
-        load_x(0, 0, WIDE[0])
-        load_x(0, 0, WIDE[1])
+        for chunk in CHUNKS[0, 0]:
+            load_x(0, 0, chunk)
         nc.sync.dma_start(bias_col[:], bi.rearrange("o (p c) -> (o p) c", c=PACK))
         nc.sync.dma_start(lists["b"][:], offs2)
         nc.sync.dma_start(lists["a"][:], offs)
-        load_x(0, 1, WIDE[0])
-        load_x(0, 1, WIDE[1])
-        load_scales(0)
-        load_scales(1)
-        load_x(1, 0, WIDE[0])
-        load_x(1, 0, WIDE[1])
-        load_scales(2)
-        load_scales(3)
-        load_x(1, 1, LAST[0])
-        load_words("a", 0)
-        load_x(1, 1, LAST[1])
-        load_x(1, 1, LAST[2])
+        for i, chunk in enumerate(CHUNKS[0, 1]):
+            load_x(0, 1, chunk)
+            load_scales(i)
+        for i, chunk in enumerate(CHUNKS[1, 0]):
+            load_x(1, 0, chunk)
+            if i < 2:
+                load_scales(2 + i)
+        for i, chunk in enumerate(CHUNKS[1, 1]):
+            load_x(1, 1, chunk)
+            if i == 1:
+                load_words("a", 0)
         load_words("b", 0)
         load_words("b", 1)
         load_words("a", 1)
@@ -148,22 +154,22 @@ def tile_moe_experts_by_agreement_pl_kernel(tc, xt, wa_words, wa_scales, wb_word
 
         for g in range(PASSES):
             for u in range(2):
-                for chunk in LAST if (g, u) == (1, 1) else WIDE:
+                for chunk in CHUNKS[g, u]:
                     cast_x(g, u, chunk)
                 gather("b", g, u)
                 gather("a", g, u)
             if g == 0:
-                weave("a", 0)
-                weave("b", 0)
+                weave("a", 0, 0)
+                weave("b", 0, 0)
                 quantize("a", 0, 0, J)
                 quantize("b", 0, 0, J)
                 for s in "ab":
                     for t in range(PACK):
                         product(s, 0, t)
-        weave("b", 1)
-        weave("a", 1)
+        weave("b", 1, P)
         quantize("b", 1, 0, J // 2)
         quantize("b", 1, J // 2, J)
+        weave("a", 1, WEAVE_SCALAR)
         for t in range(PACK):
             product("b", 1, t)
         quantize("a", 1, 0, J)
@@ -178,10 +184,13 @@ def tile_moe_experts_by_agreement_pl_kernel(tc, xt, wa_words, wa_scales, wb_word
         gate = keep.tile([P, PACK], F32, name="gate")
         for t in range(PACK):
             nc.vector.tensor_tensor(b_rows[t][:], acc["b", t][:], bias[:], ALU.add)
-            nc.gpsimd.tensor_tensor(bias_b[t][:], b_rows[t][:], bias[:], ALU.mult)
-            nc.scalar.activation(bias_b[t][:], bias_b[t][:], ACT.Copy, scale=2.0 / N, accum_out=sum_bias_b[:, t : t + 1])
+            if t < PACK - 1:
+                nc.gpsimd.tensor_tensor(bias_b[t][:], b_rows[t][:], bias[:], ALU.mult)
+                nc.scalar.activation(bias_b[t][:], bias_b[t][:], ACT.Copy, scale=2.0 / N, accum_out=sum_bias_b[:, t : t + 1])
         for t in range(PACK):
             nc.vector.scalar_tensor_tensor(y[:, t, :], acc["a", t][:], 2.0 / N, b_rows[t][:], ALU.mult, ALU.mult, accum_out=sum_ab[:, t : t + 1])
+            if t == PACK - 1:
+                nc.vector.scalar_tensor_tensor(bias_b[t][:], b_rows[t][:], 2.0 / N, bias[:], ALU.mult, ALU.mult, accum_out=sum_bias_b[:, t : t + 1])
             nc.scalar.activation(gate[:, t : t + 1], sum_ab[:, t : t + 1], ACT.Tanh, bias=sum_bias_b[:, t : t + 1])
 
         y_bf = keep.tile([P, N * PACK], BF16, name="y_bf", align_bytes=64)
@@ -200,7 +209,8 @@ def tile_moe_experts_by_agreement_pl_kernel(tc, xt, wa_words, wa_scales, wb_word
             if h == 0:
                 nc.scalar.activation(dst, src, ACT.Copy)
             else:
-                nc.vector.tensor_copy(dst, src)
+                nc.scalar.activation(dst[:, :24], src[:, :24], ACT.Copy)
+                nc.vector.tensor_copy(dst[:, 24:], src[:, 24:])
         for h in range(2):
             cols = slice(h * HALF, (h + 1) * HALF)
             nc.vector.quantize_mx(out=y_codes[:, cols].bitcast(FP8X4), scales=y_scales[:, cols], in_=y_bf[:, PACK * h * HALF : PACK * (h + 1) * HALF])

@@ -25,8 +25,8 @@ HALF = N // 2
 CHUNKS = {
     (0, 0): [(0, 2048, 704)],
     (0, 1): [(0, 1024, 1024), (1024, 1024, 352)],
-    (1, 0): [(0, 512, 512), (512, 512, 512), (1024, 512, 512), (1536, 512, 512)],
-    (1, 1): [(0, 512, 512), (512, 512, 512), (1024, 768, 320), (1792, 256, 0)],
+    (1, 0): [(0, 1024, 1024), (1024, 1024, 832)],
+    (1, 1): [(0, 1024, 1024), (1024, 768, 128), (1792, 256, 0)],
 }
 WEAVE_SCALAR = 88
 
@@ -68,12 +68,12 @@ def tile_moe_experts_by_agreement_pl_kernel(tc, xt, wa_words, wa_scales, wb_word
             c0, width, share = chunk
             if (g, u) not in pairs:
                 pairs[g, u] = keep.tile([P, T], F32, name="pair_%d%d" % (g, u))
-            dst = pairs[g, u][:].bitcast(BF16).rearrange("p (t e) -> p t e", e=2)
-            src = staged[g, u, c0][:].rearrange("p e t -> p t e")
+            dst = pairs[g, u][:, c0 : c0 + width].bitcast(BF16).rearrange("p (c i e) -> p c e i", i=4, e=2)
+            src = staged[g, u, c0][:].rearrange("p e (c i) -> p c e i", i=4)
             if share > 0:
-                nc.scalar.activation(dst[:, c0 : c0 + share, :], src[:, :share, :], ACT.Copy)
+                nc.scalar.activation(dst[:, : share // 4], src[:, : share // 4], ACT.Copy)
             if share < width:
-                nc.vector.tensor_copy(dst[:, c0 + share : c0 + width, :], src[:, share:, :])
+                nc.vector.tensor_copy(dst[:, share // 4 :], src[:, share // 4 :])
 
         gathered = {(s, g): keep.tile([P, 2, J], F32, name="gathered_%s%d" % (s, g)) for s in "ab" for g in range(PASSES)}
         woven = {(s, g): keep.tile([P, 2 * J], F32, name="woven_%s%d" % (s, g), align_bytes=64) for s in "ab" for g in range(PASSES)}
@@ -119,11 +119,10 @@ def tile_moe_experts_by_agreement_pl_kernel(tc, xt, wa_words, wa_scales, wb_word
             load_scales(i)
         for i, chunk in enumerate(CHUNKS[1, 0]):
             load_x(1, 0, chunk)
-            if i < 2:
-                load_scales(2 + i)
+            load_scales(2 + i)
         for i, chunk in enumerate(CHUNKS[1, 1]):
             load_x(1, 1, chunk)
-            if i == 1:
+            if i == 0:
                 load_words("a", 0)
         load_words("b", 0)
         load_words("b", 1)
@@ -133,6 +132,9 @@ def tile_moe_experts_by_agreement_pl_kernel(tc, xt, wa_words, wa_scales, wb_word
         for c in range(PACK):
             nc.tensor.transpose(spread[:, c, :], bias_col[:, c : c + 1].to_broadcast([P, P]), ident[:])
         nc.scalar.activation(bias[:].rearrange("m (p c) -> m p c", c=PACK), spread[:].rearrange("m c p -> m p c"), ACT.Copy)
+        bias_sq = keep.tile([P, N], F32, name="bias_sq")
+        sum_bias_sq = keep.tile([P, 1], F32, name="sum_bias_sq")
+        nc.vector.scalar_tensor_tensor(bias_sq[:], bias[:], 2.0 / N, bias[:], ALU.mult, ALU.mult, accum_out=sum_bias_sq[:])
 
         acc = {(s, t): psum.tile([P, N], F32, name="acc_%s%d" % (s, t), tag="%s%d" % (s, t)) for s in "ab" for t in range(PACK)}
 
@@ -181,37 +183,55 @@ def tile_moe_experts_by_agreement_pl_kernel(tc, xt, wa_words, wa_scales, wb_word
         y = keep.tile([P, PACK, N], F32, name="y")
         sum_ab = keep.tile([P, PACK], F32, name="sum_ab")
         sum_bias_b = keep.tile([P, PACK], F32, name="sum_bias_b")
+        sum_bias_b0 = keep.tile([P, 1], F32, name="sum_bias_b0")
         gate = keep.tile([P, PACK], F32, name="gate")
+        a_first = keep.tile([P, N], F32, name="a_first")
+        gated_first = keep.tile([P, N], F32, name="gated_first")
+        last = PACK - 1
         for t in range(PACK):
             nc.vector.tensor_tensor(b_rows[t][:], acc["b", t][:], bias[:], ALU.add)
-            if t < PACK - 1:
+            if t < last:
                 nc.gpsimd.tensor_tensor(bias_b[t][:], b_rows[t][:], bias[:], ALU.mult)
-                nc.scalar.activation(bias_b[t][:], bias_b[t][:], ACT.Copy, scale=2.0 / N, accum_out=sum_bias_b[:, t : t + 1])
+
+        def sum_product(t):
+            spent = b_rows[0] if t == 2 else bias_b[t]
+            nc.scalar.activation(spent[:], bias_b[t][:], ACT.Copy, scale=2.0 / N, accum_out=sum_bias_b[:, t : t + 1])
+
+        nc.scalar.activation(a_first[:], acc["a", 0][:], ACT.Copy)
+        sum_product(0)
+        sum_product(1)
         for t in range(PACK):
-            nc.vector.scalar_tensor_tensor(y[:, t, :], acc["a", t][:], 2.0 / N, b_rows[t][:], ALU.mult, ALU.mult, accum_out=sum_ab[:, t : t + 1])
-            if t == PACK - 1:
-                nc.vector.scalar_tensor_tensor(bias_b[t][:], b_rows[t][:], 2.0 / N, bias[:], ALU.mult, ALU.mult, accum_out=sum_bias_b[:, t : t + 1])
+            if t == 2:
+                sum_product(2)
+            product_out = bias_sq[:] if t == 0 else y[:, t, :]
+            nc.vector.scalar_tensor_tensor(product_out, acc["a", t][:], 2.0 / N, b_rows[t][:], ALU.mult, ALU.mult, accum_out=sum_ab[:, t : t + 1])
             nc.scalar.activation(gate[:, t : t + 1], sum_ab[:, t : t + 1], ACT.Tanh, bias=sum_bias_b[:, t : t + 1])
+            if t == 0:
+                nc.scalar.activation(gated_first[:], b_rows[0][:], ACT.Copy, scale=gate[:, 0:1])
+                nc.vector.scalar_tensor_tensor(bias_b[last][:], acc["b", last][:], 2.0 / N, bias[:], ALU.mult, ALU.mult, accum_out=sum_bias_b0[:])
+                nc.scalar.activation(sum_bias_b[:, last:], sum_bias_b0[:], ACT.Identity, bias=sum_bias_sq[:])
 
         y_bf = keep.tile([P, N * PACK], BF16, name="y_bf", align_bytes=64)
         y_codes = keep.tile([P, N], U32, name="y_codes", align_bytes=64)
         y_scales = keep.tile([P, N], U8, name="y_scales", align_bytes=64)
         out_rows = out_0.rearrange("(p t) n -> p t n", t=PACK)
         out_words = out_1[0].rearrange("p n t -> p (n t)").bitcast(I32)
+
+        nc.gpsimd.tensor_tensor(y[:, 0, :], gated_first[:], a_first[:], ALU.add)
+        nc.sync.dma_start(out=out_rows[:, 0, :], in_=y[:, 0, :])
+
+        def round_y(engine_copy, n0, n1):
+            dst = y_bf[:, PACK * n0 : PACK * n1].rearrange("p (c i t) -> p c t i", i=4, t=PACK)
+            src = y[:, :, n0:n1].rearrange("p t (c i) -> p c t i", i=4)
+            engine_copy(dst, src)
+
         for h in range(2):
             cols = slice(h * HALF, (h + 1) * HALF)
-            for t in range(PACK):
+            for t in range(1, PACK):
                 nc.vector.scalar_tensor_tensor(y[:, t, cols], b_rows[t][:, cols], gate[:, t : t + 1], acc["a", t][:, cols], ALU.mult, ALU.add)
-                if t % 2 == 1:
-                    nc.sync.dma_start(out=out_rows[:, t - 1 : t + 1, cols], in_=y[:, t - 1 : t + 1, cols])
-            dst = y_bf[:, PACK * h * HALF : PACK * (h + 1) * HALF].rearrange("p (c i t) -> p c t i", i=4, t=PACK)
-            src = y[:, :, cols].rearrange("p t (c i) -> p c t i", i=4)
-            if h == 0:
-                nc.scalar.activation(dst, src, ACT.Copy)
-            else:
-                nc.scalar.activation(dst[:, :24], src[:, :24], ACT.Copy)
-                nc.vector.tensor_copy(dst[:, 24:], src[:, 24:])
-        for h in range(2):
+            nc.sync.dma_start(out=out_rows[:, 1:, cols], in_=y[:, 1:, cols])
+            round_y(nc.scalar.copy if h == 0 else nc.vector.tensor_copy, h * HALF, (h + 1) * HALF)
+        for h in (1, 0):
             cols = slice(h * HALF, (h + 1) * HALF)
             nc.vector.quantize_mx(out=y_codes[:, cols].bitcast(FP8X4), scales=y_scales[:, cols], in_=y_bf[:, PACK * h * HALF : PACK * (h + 1) * HALF])
             nc.sync.dma_start(out=out_words[:, cols], in_=y_codes[:, cols].bitcast(I32))

from contextlib import ExitStack

import concourse.mybir as mybir
from concourse.masks import make_identity

K, T, J, N = 1024, 2048, 512, 512
FLOPS = 2 * 2 * K * J * N

F32 = mybir.dt.float32
BF16 = mybir.dt.bfloat16
I32 = mybir.dt.int32
U32 = mybir.dt.uint32
U16 = mybir.dt.uint16
U8 = mybir.dt.uint8
FP8X4 = mybir.dt.float8_e4m3fn_x4
FP4X4 = mybir.dt.float4_e2m1fn_x4
ACT = mybir.ActivationFunctionType
ALU = mybir.AluOpType

P = 128
PACK = 4
PASSES = K // (P * PACK)
HALF = N // 2

CHUNKS = {
    (0, 0): [(0, 2048, 704)],
    (0, 1): [(0, 1024, 1024), (1024, 1024, 352)],
    (1, 0): [(0, 1024, 1024), (1024, 1024, 832)],
    (1, 1): [(0, 1024, 1024), (1024, 768, 128), (1792, 256, 0)],
}
WEAVE_SCALAR = 88


def tile_moe_experts_by_agreement_pl_kernel(tc, xt, wa_words, wa_scales, wb_words, wb_scales, bi, offs, offs2, out_0, out_1, out_2):
    nc = tc.nc
    with ExitStack() as ctx:
        keep = ctx.enter_context(tc.tile_pool(name="keep", bufs=1))
        psum = ctx.enter_context(tc.psum_pool(name="psum", bufs=1))

        x_rows = xt.rearrange("(g p u e) t -> g u p e t", g=PASSES, p=P, u=2, e=2)

        lists = {"a": keep.tile([P, J // 16], U16, name="list_a"), "b": keep.tile([P, J // 16], U16, name="list_b")}
        wa = keep.tile([P, PASSES, 2 * N], U8, name="wa", align_bytes=64)
        wb = keep.tile([P, PASSES, N], U32, name="wb", align_bytes=64)
        sa = keep.tile([P, PASSES, N], U8, name="sa", align_bytes=64)
        sb = keep.tile([P, N], U8, name="sb", align_bytes=64)
        bias_col = keep.tile([P, PACK], F32, name="bias_col")
        bias = keep.tile([P, N], F32, name="bias")
        ident = keep.tile([P, P], F32, name="ident")
        warm = keep.tile([P, 8], F32, name="warm")

        nc.vector.memset(warm[:], 0.0)
        nc.scalar.activation(warm[:, 0:1], warm[:, 1:2], ACT.Tanh)
        nc.vector.memset(sa[:].rearrange("p g n -> p (g n)").bitcast(I32), 0)
        nc.vector.memset(sb[:].bitcast(I32), 0)
        make_identity(nc, ident[:])

        pairs = {}
        staged = {}

        def load_x(g, u, chunk):
            c0, width, share = chunk
            raw = keep.tile([P, 2, width], F32, name="raw_%d%d_%d" % (g, u, c0))
            nc.sync.dma_start(out=raw[:], in_=x_rows[g, u][:, :, c0 : c0 + width])
            staged[g, u, c0] = raw

        def cast_x(g, u, chunk):
            c0, width, share = chunk
            if (g, u) not in pairs:
                pairs[g, u] = keep.tile([P, T], F32, name="pair_%d%d" % (g, u))
            dst = pairs[g, u][:, c0 : c0 + width].bitcast(BF16).rearrange("p (c i e) -> p c e i", i=4, e=2)
            src = staged[g, u, c0][:].rearrange("p e (c i) -> p c e i", i=4)
            if share > 0:
                nc.scalar.activation(dst[:, : share // 4], src[:, : share // 4], ACT.Copy)
            if share < width:
                nc.vector.tensor_copy(dst[:, share // 4 :], src[:, share // 4 :])

        gathered = {(s, g): keep.tile([P, 2, J], F32, name="gathered_%s%d" % (s, g)) for s in "ab" for g in range(PASSES)}
        woven = {(s, g): keep.tile([P, 2 * J], F32, name="woven_%s%d" % (s, g), align_bytes=64) for s in "ab" for g in range(PASSES)}
        codes = {(s, g): keep.tile([P, J], U32, name="codes_%s%d" % (s, g), align_bytes=64) for s in "ab" for g in range(PASSES)}
        scales = {(s, g): keep.tile([P, J], U8, name="scales_%s%d" % (s, g), align_bytes=64) for s in "ab" for g in range(PASSES)}

        def gather(s, g, u):
            nc.vector.tensor_copy(gathered[s, g][:, u, :], pairs[g, u][:].indirect(lists[s][:]))

        def weave(s, g, m_scalar):
            dst = woven[s, g][:].rearrange("p (t m u) -> p m u t", t=PACK, u=2)
            src = gathered[s, g][:].rearrange("p u (m t) -> p m u t", t=PACK)
            if m_scalar > 0:
                nc.scalar.copy(dst[:, :m_scalar], src[:, :m_scalar])
            if m_scalar < P:
                nc.vector.tensor_copy(dst[:, m_scalar:], src[:, m_scalar:])

        def quantize(s, g, c0, c1):
            nc.vector.quantize_mx(
                out=codes[s, g][:, c0:c1].bitcast(FP8X4),
                scales=scales[s, g][:, c0:c1],
                in_=woven[s, g][:].bitcast(BF16)[:, PACK * c0 : PACK * c1],
            )

        def load_words(s, g):
            if s == "a":
                nc.sync.dma_start(out=wa[:, g, :].bitcast(I32), in_=wa_words[g].bitcast(I32))
            else:
                nc.sync.dma_start(out=wb[:, g, :].bitcast(I32), in_=wb_words[g].rearrange("p n t -> p (n t)").bitcast(I32))

        def load_scales(q):
            rows = slice(4 * q, 4 * q + 4)
            nc.sync.dma_start(out=sa[32 * q : 32 * q + 4, :, :].bitcast(I32), in_=wa_scales[:, rows, :].rearrange("g r n -> r g n").bitcast(I32))
            nc.sync.dma_start(out=sb[32 * q + 4 : 32 * q + 12, :].bitcast(I32), in_=wb_scales[:, rows, :].bitcast(I32))

        for chunk in CHUNKS[0, 0]:
            load_x(0, 0, chunk)
        nc.sync.dma_start(bias_col[:], bi.rearrange("o (p c) -> (o p) c", c=PACK))
        nc.sync.dma_start(lists["b"][:], offs2)
        nc.sync.dma_start(lists["a"][:], offs)
        for i, chunk in enumerate(CHUNKS[0, 1]):
            load_x(0, 1, chunk)
            load_scales(i)
        for i, chunk in enumerate(CHUNKS[1, 0]):
            load_x(1, 0, chunk)
            load_scales(2 + i)
        for i, chunk in enumerate(CHUNKS[1, 1]):
            load_x(1, 1, chunk)
            if i == 0:
                load_words("a", 0)
        load_words("b", 0)
        load_words("b", 1)
        load_words("a", 1)

        spread = psum.tile([P, PACK, P], F32, name="spread", tag="a0")
        for c in range(PACK):
            nc.tensor.transpose(spread[:, c, :], bias_col[:, c : c + 1].to_broadcast([P, P]), ident[:])
        nc.scalar.activation(bias[:].rearrange("m (p c) -> m p c", c=PACK), spread[:].rearrange("m c p -> m p c"), ACT.Copy)
        bias_sq = keep.tile([P, N], F32, name="bias_sq")
        sum_bias_sq = keep.tile([P, 1], F32, name="sum_bias_sq")
        nc.vector.scalar_tensor_tensor(bias_sq[:], bias[:], 2.0 / N, bias[:], ALU.mult, ALU.mult, accum_out=sum_bias_sq[:])

        acc = {(s, t): psum.tile([P, N], F32, name="acc_%s%d" % (s, t), tag="%s%d" % (s, t)) for s in "ab" for t in range(PACK)}

        def product(s, g, t):
            cols = slice(t * P, (t + 1) * P)
            if s == "a":
                rhs, rhs_scale = wa[:, g, :].bitcast(FP4X4), sa[:, g, :]
            else:
                rhs, rhs_scale = wb[:, g, :].bitcast(FP8X4), sb[4 + 4 * g :, :]
            nc.tensor.matmul_mx(
                out=acc[s, t][:],
                lhsT=codes[s, g][:, cols].bitcast(FP8X4),
                lhsT_scale=scales[s, g][:, cols],
                rhs=rhs,
                rhs_scale=rhs_scale,
                start=(g == 0),
                stop=(g == PASSES - 1),
            )

        for g in range(PASSES):
            for u in range(2):
                for chunk in CHUNKS[g, u]:
                    cast_x(g, u, chunk)
                gather("b", g, u)
                gather("a", g, u)
            if g == 0:
                weave("a", 0, 0)
                weave("b", 0, 0)
                quantize("a", 0, 0, J)
                quantize("b", 0, 0, J)
                for s in "ab":
                    for t in range(PACK):
                        product(s, 0, t)
        weave("b", 1, P)
        quantize("b", 1, 0, J // 2)
        quantize("b", 1, J // 2, J)
        weave("a", 1, WEAVE_SCALAR)
        for t in range(PACK):
            product("b", 1, t)
        quantize("a", 1, 0, J)
        for t in range(PACK):
            product("a", 1, t)

        b_rows = [keep.tile([P, N], F32, name="b_rows%d" % t) for t in range(PACK)]
        bias_b = [keep.tile([P, N], F32, name="bias_b%d" % t) for t in range(PACK)]
        y = keep.tile([P, PACK, N], F32, name="y")
        sum_ab = keep.tile([P, PACK], F32, name="sum_ab")
        sum_bias_b = keep.tile([P, PACK], F32, name="sum_bias_b")
        sum_bias_b0 = keep.tile([P, 1], F32, name="sum_bias_b0")
        gate = keep.tile([P, PACK], F32, name="gate")
        a_first = keep.tile([P, N], F32, name="a_first")
        gated_first = keep.tile([P, N], F32, name="gated_first")
        last = PACK - 1
        for t in range(PACK):
            nc.vector.tensor_tensor(b_rows[t][:], acc["b", t][:], bias[:], ALU.add)
            if t < last:
                nc.gpsimd.tensor_tensor(bias_b[t][:], b_rows[t][:], bias[:], ALU.mult)

        def sum_product(t):
            spent = b_rows[0] if t == 2 else bias_b[t]
            nc.scalar.activation(spent[:], bias_b[t][:], ACT.Copy, scale=2.0 / N, accum_out=sum_bias_b[:, t : t + 1])

        nc.scalar.activation(a_first[:], acc["a", 0][:], ACT.Copy)
        sum_product(0)
        sum_product(1)
        for t in range(PACK):
            if t == 2:
                sum_product(2)
            product_out = bias_sq[:] if t == 0 else y[:, t, :]
            nc.vector.scalar_tensor_tensor(product_out, acc["a", t][:], 2.0 / N, b_rows[t][:], ALU.mult, ALU.mult, accum_out=sum_ab[:, t : t + 1])
            nc.scalar.activation(gate[:, t : t + 1], sum_ab[:, t : t + 1], ACT.Tanh, bias=sum_bias_b[:, t : t + 1])
            if t == 0:
                nc.scalar.activation(gated_first[:], b_rows[0][:], ACT.Copy, scale=gate[:, 0:1])
                nc.vector.scalar_tensor_tensor(bias_b[last][:], acc["b", last][:], 2.0 / N, bias[:], ALU.mult, ALU.mult, accum_out=sum_bias_b0[:])
                nc.scalar.activation(sum_bias_b[:, last:], sum_bias_b0[:], ACT.Identity, bias=sum_bias_sq[:])

        y_bf = keep.tile([P, N * PACK], BF16, name="y_bf", align_bytes=64)
        y_codes = keep.tile([P, N], U32, name="y_codes", align_bytes=64)
        y_scales = keep.tile([P, N], U8, name="y_scales", align_bytes=64)
        out_rows = out_0.rearrange("(p t) n -> p t n", t=PACK)
        out_words = out_1[0].rearrange("p n t -> p (n t)").bitcast(I32)

        nc.gpsimd.tensor_tensor(y[:, 0, :], gated_first[:], a_first[:], ALU.add)
        nc.sync.dma_start(out=out_rows[:, 0, :], in_=y[:, 0, :])

        def round_y(engine_copy, n0, n1):
            dst = y_bf[:, PACK * n0 : PACK * n1].rearrange("p (c i t) -> p c t i", i=4, t=PACK)
            src = y[:, :, n0:n1].rearrange("p t (c i) -> p c t i", i=4)
            engine_copy(dst, src)

        for h in range(2):
            cols = slice(h * HALF, (h + 1) * HALF)
            for t in range(1, PACK):
                nc.vector.scalar_tensor_tensor(y[:, t, cols], b_rows[t][:, cols], gate[:, t : t + 1], acc["a", t][:, cols], ALU.mult, ALU.add)
            nc.sync.dma_start(out=out_rows[:, 1:, cols], in_=y[:, 1:, cols])
            round_y(nc.scalar.copy if h == 0 else nc.vector.tensor_copy, h * HALF, (h + 1) * HALF)
        for h in (1, 0):
            cols = slice(h * HALF, (h + 1) * HALF)
            nc.vector.quantize_mx(out=y_codes[:, cols].bitcast(FP8X4), scales=y_scales[:, cols], in_=y_bf[:, PACK * h * HALF : PACK * (h + 1) * HALF])
            nc.sync.dma_start(out=out_words[:, cols], in_=y_codes[:, cols].bitcast(I32))
        for q in range(4):
            queue = nc.scalar if q % 2 == 0 else nc.sync
            queue.dma_start(out=out_2[0, 4 * q : 4 * q + 4, :].bitcast(I32), in_=y_scales[32 * q : 32 * q + 4, :].bitcast(I32))
